import numpy as np
import ml_dtypes


def mxq(x, axis, fmt="e4m3"):
    dtype, down = {"e4m3": (ml_dtypes.float8_e4m3fn, 7), "e5m2": (ml_dtypes.float8_e5m2, 14)}[fmt]
    v = np.moveaxis(np.asarray(x, np.float32).astype(ml_dtypes.bfloat16).astype(np.float64), axis, -1)
    blocks = v.reshape(v.shape[:-1] + (-1, 32))
    amax = np.abs(blocks).max(-1, keepdims=True)
    byte = np.maximum(np.where(amax > 0, np.frexp(amax)[1] - 1 + 127, 0) - down, 1)
    scale = np.exp2(byte - 127.0)
    codes = (blocks / scale).astype(np.float32).astype(dtype).astype(np.float64)
    return np.moveaxis((codes * scale).reshape(v.shape), -1, axis)


WIDE = False


def mx_kscale(k):
    if not WIDE:
        return np.ones(k)
    levels = np.array([10, -10, 5, -5, 0])
    if k % 512:
        return np.exp2(np.random.permutation(np.resize(levels, k // 32))).repeat(32)
    a = np.empty((k // 512, 16))
    for p in range(k // 512):
        a[p, :8] = np.random.permutation(np.resize(levels, 8))
        for g in range(8):
            far = levels[np.abs(levels - a[p, g]) >= 10]
            a[p, g + 8] = far[np.random.randint(len(far))]
    return np.exp2(a.ravel()).repeat(32)


def f64(x):
    return np.asarray(x).astype(np.float64)


def striped8(idx):
    return np.asarray(idx).reshape(8, -1, 16).transpose(0, 2, 1).reshape(128, -1).astype(np.uint16)


def unstriped8(offs):
    return offs.reshape(8, 16, -1).transpose(0, 2, 1).reshape(8, -1).astype(np.int64)


def pick8(x, idx, run):
    r = np.arange(len(x))
    return x[r[:, None], idx[r % (8 * run) // run]]


E2M1 = np.array([0.0, 0.5, 1.0, 1.5, 2.0, 3.0, 4.0, 6.0, -0.0, -0.5, -1.0, -1.5, -2.0, -3.0, -4.0, -6.0])


def pack_weight(w, fmt):
    k, n = w.shape
    w = f64(np.asarray(w, np.float32).astype(ml_dtypes.bfloat16)).reshape(k // 32, 32, n)
    amax = np.abs(w).max(1)
    if fmt == "e4m3":
        byte = np.frexp(amax)[1] - 1 + 127 - 7
    else:
        mant, ex = np.frexp(amax / 6.0)
        byte = np.where(mant > 0.5, ex, ex - 1) + 127
    byte = np.clip(np.where(amax > 0, byte, 1), 1, 254)
    scaled = (w * np.exp2(127.0 - byte)[:, None, :]).reshape(k, n).astype(np.float32)
    by_word = np.ascontiguousarray(scaled.reshape(k // 512, 128, 4, n).transpose(0, 1, 3, 2))
    if fmt == "e4m3":
        words = by_word.astype(ml_dtypes.float8_e4m3fn).view(np.uint8)
    else:
        c = by_word.astype(ml_dtypes.float4_e2m1fn).view(np.uint8) & 0xF
        words = (c[..., 0::2] | (c[..., 1::2] << 4)).reshape(k // 512, 128, 2 * n)
    return np.ascontiguousarray(words), np.ascontiguousarray(byte.astype(np.uint8).reshape(k // 512, 16, n))


def unpack_weight(words, scales, fmt):
    g, _, n = scales.shape
    words = np.ascontiguousarray(words).reshape(g, 128, n, -1)
    if fmt == "e4m3":
        vals = words.view(ml_dtypes.float8_e4m3fn).astype(np.float64)
    else:
        nib = np.empty((g, 128, n, 4), np.uint8)
        nib[..., 0::2] = words & 0xF
        nib[..., 1::2] = words >> 4
        vals = E2M1[nib]
    vals = vals * np.repeat(np.exp2(scales.astype(np.float64) - 127.0), 8, axis=1)[..., None]
    return vals.transpose(0, 1, 3, 2).reshape(g * 512, n)


D, T, I, Q = 512, 1024, 512, 128


def setup_inputs():
    n = np.random.standard_normal
    idx = np.stack([np.random.permutation(T)[:I] for _ in range(8)])
    idx2 = np.stack([np.random.permutation(T)[:I] for _ in range(8)])
    fd = mx_kscale(D)
    keysp = pack_weight(n((D, T)) / fd[:, None], "e2m1")
    return {
        "query": (n((D, Q)) * 0.9 / np.sqrt(D) * fd[:, None]).astype(np.float32),
        "query2": (n((D, Q)) * 0.9 / np.sqrt(D) * fd[:, None]).astype(np.float32),
        "keys_words": keysp[0],
        "keys_scales": keysp[1],
        "lam": (np.random.uniform(0.5, 1.5, (Q, 1))).astype(np.float32),
        "damp": (np.random.uniform(1.0, 4.0, (Q, 1))).astype(np.float32),
        "old": (np.random.uniform(0.0, 2.0, (Q, T))).astype(np.float32),
        "fade": (np.random.uniform(0.3, 0.9, (Q, 1))).astype(np.float32),
        "offs": striped8(idx),
        "offs2": striped8(idx2),
    }


def reference(query, query2, keys_words, keys_scales, lam, damp, old, fade, offs, offs2):
    idx = unstriped8(offs)
    idx2 = unstriped8(offs2)
    keysu = unpack_weight(keys_words, keys_scales, "e2m1")
    queryq = mxq(f64(query), 0, "e4m3")
    a = queryq.T @ keysu
    query2q = mxq(f64(query2), 0, "e4m3")
    b = query2q.T @ keysu
    s = pick8(a, idx, 16) + pick8(a, idx2, 16) * np.tanh(pick8(b, idx, 16)) * f64(lam)
    p = np.exp(s - np.max(s, axis=1, keepdims=True))
    r = p / np.sum(p, axis=1, keepdims=True) * 512.0
    u0 = np.log(r * f64(damp) + 1.0)
    w = u0 / np.sum(u0, axis=1, keepdims=True)
    ws = w * 512.0
    wf = np.zeros((Q, T))
    wf[np.arange(Q)[:, None], idx[np.arange(Q) % 128 // 16]] = ws
    y = f64(old) * f64(fade) + wf
    return y

@@ -1,0 +1,142 @@
+from contextlib import ExitStack
+
+import concourse.mybir as mybir
+
+D, T, I, Q = 512, 1024, 512, 128
+P = 128
+PACK = 4
+N_MM = 256
+N_OUT = 256
+
+FLOPS = 2 * 2 * D * T * Q
+
+F32 = mybir.dt.float32
+BF16 = mybir.dt.bfloat16
+I32 = mybir.dt.int32
+U32 = mybir.dt.uint32
+U16 = mybir.dt.uint16
+U8 = mybir.dt.uint8
+FP8X4 = mybir.dt.float8_e4m3fn_x4
+FP4X4 = mybir.dt.float4_e2m1fn_x4
+ACT = mybir.ActivationFunctionType
+ALU = mybir.AluOpType
+
+
+def quantize_query(nc, pool, raw, name):
+    grouped = pool.tile([P, Q, PACK], BF16, name=name + "_grouped", align_bytes=64)
+    codes = pool.tile([P, Q], U32, name=name + "_codes", align_bytes=64)
+    scales = pool.tile([P, Q], U8, name=name + "_scales", align_bytes=64)
+    nc.vector.tensor_copy(
+        out=grouped[:].rearrange("p (c i) t -> p c t i", i=4),
+        in_=raw[:].rearrange("p t (c i) -> p c t i", i=4),
+    )
+    nc.vector.quantize_mx(
+        out=codes[:].bitcast(FP8X4),
+        scales=scales[:],
+        in_=grouped[:].rearrange("p w t -> p (w t)"),
+    )
+    return codes, scales
+
+
+def tile_attend_turnedby_dampened_counts_heads_kernel(
+    tc, query, query2, keys_words, keys_scales, lam, damp, old, fade, offs, offs2, out
+):
+    nc = tc.nc
+    with ExitStack() as ctx:
+        pool = ctx.enter_context(tc.tile_pool(name="held", bufs=1))
+        psum = ctx.enter_context(tc.psum_pool(name="psum", bufs=1))
+
+        list1 = pool.tile([P, I // 16], U16, name="list1")
+        list2 = pool.tile([P, I // 16], U16, name="list2")
+        q2_raw = pool.tile([P, PACK, Q], F32, name="q2_raw", tag="staged")
+        q_raw = pool.tile([P, PACK, Q], F32, name="q_raw")
+        words = pool.tile([P, 2 * T], U8, name="words", align_bytes=64)
+        key_scales = pool.tile([P, T], U8, name="key_scales", align_bytes=64)
+        lam_sb = pool.tile([P, 1], F32, name="lam_sb")
+        damp_sb = pool.tile([P, 1], F32, name="damp_sb")
+        fade_sb = pool.tile([P, 1], F32, name="fade_sb")
+        placed = pool.tile([P, T], F32, name="placed")
+
+        nc.sync.dma_start(out=q2_raw[:], in_=query2.rearrange("(p t) w -> p t w", t=PACK))
+        for quad in range(4):
+            nc.scalar.dma_start(
+                out=key_scales[32 * quad : 32 * quad + 4, :].bitcast(I32),
+                in_=keys_scales[0, 4 * quad : 4 * quad + 4, :].bitcast(I32),
+            )
+        nc.sync.dma_start(out=words[:].bitcast(I32), in_=keys_words[0].bitcast(I32))
+        nc.sync.dma_start(out=q_raw[:], in_=query.rearrange("(p t) w -> p t w", t=PACK))
+        nc.sync.dma_start(list1[:], offs)
+        nc.sync.dma_start(list2[:], offs2)
+        nc.sync.dma_start(out=lam_sb[:], in_=lam)
+        nc.sync.dma_start(out=damp_sb[:], in_=damp)
+        nc.sync.dma_start(out=fade_sb[:], in_=fade)
+        nc.vector.memset(placed[:], 0.0)
+
+        a_sb = pool.tile([P, T], F32, name="a_sb")
+        b_sb = pool.tile([P, T], F32, name="b_sb")
+
+        def scores(raw, name, dest, copy):
+            codes, scales = quantize_query(nc, pool, raw, name)
+            for n0 in range(0, T, N_MM):
+                bank = psum.tile([P, N_MM], F32, name="%s_bank%d" % (name, n0 // N_MM))
+                nc.tensor.matmul_mx(
+                    out=bank[:],
+                    lhsT=codes[:].bitcast(FP8X4),
+                    lhsT_scale=scales[:],
+                    rhs=words[:, 2 * n0 : 2 * (n0 + N_MM)].bitcast(FP4X4),
+                    rhs_scale=key_scales[:, n0 : n0 + N_MM],
+                    start=True,
+                    stop=True,
+                )
+                copy(out=dest[:, n0 : n0 + N_MM], in_=bank[:])
+
+        scores(q2_raw, "q2", b_sb, nc.scalar.copy)
+        old_sb = pool.tile([P, T], F32, name="old_sb", tag="staged")
+        nc.sync.dma_start(out=old_sb[:], in_=old)
+        scores(q_raw, "q", a_sb, nc.vector.tensor_copy)
+
+        halves = [slice(0, I // 2), slice(I // 2, I)]
+        list_halves = [slice(0, I // 32), slice(I // 32, I // 16)]
+        b_at1 = pool.tile([P, I], F32, name="b_at1")
+        turn = pool.tile([P, I], F32, name="turn")
+        a_at2 = pool.tile([P, I], F32, name="a_at2")
+        term = pool.tile([P, I], F32, name="term")
+        s = pool.tile([P, I], F32, name="s")
+        neg_max = pool.tile([P, 1], F32, name="neg_max")
+        for h, lh in zip(halves, list_halves):
+            nc.scalar.activation(b_at1[:, h], b_sb[:].indirect(list1[:, lh]), ACT.Copy)
+        for h in halves:
+            nc.scalar.activation(turn[:, h], b_at1[:, h], ACT.Tanh)
+        for h, lh in zip(halves, list_halves):
+            nc.scalar.activation(b_at1[:, h], a_sb[:].indirect(list1[:, lh]), ACT.Copy)
+        for h, lh in zip(halves, list_halves):
+            nc.vector.tensor_copy(a_at2[:, h], a_sb[:].indirect(list2[:, lh]))
+        for h in halves:
+            nc.vector.scalar_tensor_tensor(term[:, h], turn[:, h], lam_sb[:], a_at2[:, h], ALU.mult, ALU.mult)
+        for h in halves:
+            nc.vector.tensor_tensor(s[:, h], term[:, h], b_at1[:, h], ALU.add)
+        nc.vector.tensor_reduce(neg_max[:], s[:], mybir.AxisListType.X, ALU.max, negate=True)
+
+        p = pool.tile([P, I], F32, name="p")
+        p_sum = pool.tile([P, 1], F32, name="p_sum")
+        p_inv = pool.tile([P, 1], F32, name="p_inv")
+        gain = pool.tile([P, 1], F32, name="gain")
+        nc.scalar.activation(p[:], s[:], ACT.Exp, bias=neg_max[:], accum_out=p_sum[:])
+        nc.vector.reciprocal(p_inv[:], p_sum[:])
+        nc.vector.tensor_scalar(gain[:], p_inv[:], damp_sb[:], float(I), ALU.mult, ALU.mult)
+
+        part = pool.tile([P, I], F32, name="part")
+        part_sum = pool.tile([P, 1], F32, name="part_sum")
+        part_inv = pool.tile([P, 1], F32, name="part_inv")
+        ws = pool.tile([P, I], F32, name="ws")
+        nc.scalar.activation(part[:], p[:], ACT.Ln, bias=1.0, scale=gain[:], accum_out=part_sum[:])
+        nc.vector.reciprocal(part_inv[:], part_sum[:])
+        nc.vector.tensor_scalar(ws[:], part[:], part_inv[:], float(I), ALU.mult, ALU.mult)
+        nc.vector.tensor_copy(placed[:].indirect(list1[:]), ws[:])
+
+        for j, t0 in enumerate(range(0, T, N_OUT)):
+            cols = slice(t0, t0 + N_OUT)
+            result = pool.tile([P, N_OUT], F32, name="result%d" % j)
+            nc.vector.scalar_tensor_tensor(result[:], old_sb[:, cols], fade_sb[:], placed[:, cols], ALU.mult, ALU.add)
+            queue = nc.sync if j % 2 == 0 else nc.scalar
+            queue.dma_start(out=out[:, cols], in_=result[:])

@@ -50,7 +50,7 @@ def tile_attend_turnedby_dampened_counts_heads_kernel(
         list2 = pool.tile([P, I // 16], U16, name="list2")
         q2_raw = pool.tile([P, PACK, Q], F32, name="q2_raw", tag="staged")
         q_raw = pool.tile([P, PACK, Q], F32, name="q_raw")
-        words = pool.tile([P, 2 * T], U8, name="words", align_bytes=64)
+        words = [pool.tile([P, T], U8, name="words%d" % j, align_bytes=64) for j in range(2)]
         key_scales = pool.tile([P, T], U8, name="key_scales", align_bytes=64)
         lam_sb = pool.tile([P, 1], F32, name="lam_sb")
         damp_sb = pool.tile([P, 1], F32, name="damp_sb")
@@ -63,8 +63,9 @@ def tile_attend_turnedby_dampened_counts_heads_kernel(
                 out=key_scales[32 * quad : 32 * quad + 4, :].bitcast(I32),
                 in_=keys_scales[0, 4 * quad : 4 * quad + 4, :].bitcast(I32),
             )
-        nc.sync.dma_start(out=words[:].bitcast(I32), in_=keys_words[0].bitcast(I32))
+        nc.sync.dma_start(out=words[0][:].bitcast(I32), in_=keys_words[0, :, 0:T].bitcast(I32))
         nc.sync.dma_start(out=q_raw[:], in_=query.rearrange("(p t) w -> p t w", t=PACK))
+        nc.sync.dma_start(out=words[1][:].bitcast(I32), in_=keys_words[0, :, T : 2 * T].bitcast(I32))
         nc.sync.dma_start(list1[:], offs)
         nc.sync.dma_start(list2[:], offs2)
         nc.sync.dma_start(out=lam_sb[:], in_=lam)
@@ -83,7 +84,7 @@ def tile_attend_turnedby_dampened_counts_heads_kernel(
                     out=bank[:],
                     lhsT=codes[:].bitcast(FP8X4),
                     lhsT_scale=scales[:],
-                    rhs=words[:, 2 * n0 : 2 * (n0 + N_MM)].bitcast(FP4X4),
+                    rhs=words[2 * n0 // T][:, 2 * n0 % T : 2 * n0 % T + 2 * N_MM].bitcast(FP4X4),
                     rhs_scale=key_scales[:, n0 : n0 + N_MM],
                     start=True,
                     stop=True,
@@ -115,14 +116,29 @@ def tile_attend_turnedby_dampened_counts_heads_kernel(
             nc.vector.scalar_tensor_tensor(term[:, h], turn[:, h], lam_sb[:], a_at2[:, h], ALU.mult, ALU.mult)
         for h in halves:
             nc.vector.tensor_tensor(s[:, h], term[:, h], b_at1[:, h], ALU.add)
-        nc.vector.tensor_reduce(neg_max[:], s[:], mybir.AxisListType.X, ALU.max, negate=True)
-
+        half_neg_max = pool.tile([P, 2], F32, name="half_neg_max")
+        half_sum = pool.tile([P, 2], F32, name="half_sum")
+        rescale = pool.tile([P, 2], F32, name="rescale")
+        rescaled_sum = pool.tile([P, 2], F32, name="rescaled_sum")
+        e = pool.tile([P, I], F32, name="e")
         p = pool.tile([P, I], F32, name="p")
         p_sum = pool.tile([P, 1], F32, name="p_sum")
         p_inv = pool.tile([P, 1], F32, name="p_inv")
         gain = pool.tile([P, 1], F32, name="gain")
-        nc.scalar.activation(p[:], s[:], ACT.Exp, bias=neg_max[:], accum_out=p_sum[:])
+        for j, h in enumerate(halves):
+            nc.vector.tensor_reduce(half_neg_max[:, j : j + 1], s[:, h], mybir.AxisListType.X, ALU.max, negate=True)
+        nc.vector.tensor_tensor(neg_max[:], half_neg_max[:, 0:1], half_neg_max[:, 1:2], ALU.min)
+        for j, h in enumerate(halves):
+            nc.scalar.activation(
+                e[:, h], s[:, h], ACT.Exp, bias=half_neg_max[:, j : j + 1], accum_out=half_sum[:, j : j + 1]
+            )
+        nc.scalar.activation(rescale[:], half_neg_max[:], ACT.Exp, bias=neg_max[:], scale=-1.0)
+        nc.vector.scalar_tensor_tensor(
+            rescaled_sum[:], half_sum[:], 1.0, rescale[:], ALU.mult, ALU.mult, accum_out=p_sum[:]
+        )
+        nc.vector.tensor_scalar(p[:, halves[0]], e[:, halves[0]], rescale[:, 0:1], None, ALU.mult)
         nc.vector.reciprocal(p_inv[:], p_sum[:])
+        nc.vector.tensor_scalar(p[:, halves[1]], e[:, halves[1]], rescale[:, 1:2], None, ALU.mult)
         nc.vector.tensor_scalar(gain[:], p_inv[:], damp_sb[:], float(I), ALU.mult, ALU.mult)
 
         part = pool.tile([P, I], F32, name="part")
@@ -134,9 +150,10 @@ def tile_attend_turnedby_dampened_counts_heads_kernel(
         nc.vector.tensor_scalar(ws[:], part[:], part_inv[:], float(I), ALU.mult, ALU.mult)
         nc.vector.tensor_copy(placed[:].indirect(list1[:]), ws[:])
 
-        for j, t0 in enumerate(range(0, T, N_OUT)):
-            cols = slice(t0, t0 + N_OUT)
-            result = pool.tile([P, N_OUT], F32, name="result%d" % j)
+        edges = [0, 128, 384, 640, 896, 1024]
+        for j in range(len(edges) - 1):
+            cols = slice(edges[j], edges[j + 1])
+            result = pool.tile([P, edges[j + 1] - edges[j]], F32, name="result%d" % j)
             nc.vector.scalar_tensor_tensor(result[:], old_sb[:, cols], fade_sb[:], placed[:, cols], ALU.mult, ALU.add)
             queue = nc.sync if j % 2 == 0 else nc.scalar
             queue.dma_start(out=out[:, cols], in_=result[:])

@@ -22,14 +22,15 @@ ACT = mybir.ActivationFunctionType
 ALU = mybir.AluOpType
 
 
-def quantize_query(nc, pool, raw, name):
+def quantize_query(nc, pool, raw, name, shares):
     grouped = pool.tile([P, Q, PACK], BF16, name=name + "_grouped", align_bytes=64)
     codes = pool.tile([P, Q], U32, name=name + "_codes", align_bytes=64)
     scales = pool.tile([P, Q], U8, name=name + "_scales", align_bytes=64)
-    nc.vector.tensor_copy(
-        out=grouped[:].rearrange("p (c i) t -> p c t i", i=4),
-        in_=raw[:].rearrange("p t (c i) -> p c t i", i=4),
-    )
+    for copy, cols in shares:
+        copy(
+            out=grouped[:, cols, :].rearrange("p (c i) t -> p c t i", i=4),
+            in_=raw[:, :, cols].rearrange("p t (c i) -> p c t i", i=4),
+        )
     nc.vector.quantize_mx(
         out=codes[:].bitcast(FP8X4),
         scales=scales[:],
@@ -76,8 +77,9 @@ def tile_attend_turnedby_dampened_counts_heads_kernel(
         a_sb = pool.tile([P, T], F32, name="a_sb")
         b_sb = pool.tile([P, T], F32, name="b_sb")
 
-        def scores(raw, name, dest, copy):
-            codes, scales = quantize_query(nc, pool, raw, name)
+        def scores(raw, name, shares):
+            codes, scales = quantize_query(nc, pool, raw, name, shares)
+            banks = []
             for n0 in range(0, T, N_MM):
                 bank = psum.tile([P, N_MM], F32, name="%s_bank%d" % (name, n0 // N_MM))
                 nc.tensor.matmul_mx(
@@ -89,33 +91,35 @@ def tile_attend_turnedby_dampened_counts_heads_kernel(
                     start=True,
                     stop=True,
                 )
-                copy(out=dest[:, n0 : n0 + N_MM], in_=bank[:])
+                banks.append(bank)
+            return banks
 
-        scores(q2_raw, "q2", b_sb, nc.scalar.copy)
+        b_banks = scores(q2_raw, "q2", [(nc.vector.tensor_copy, slice(0, Q))])
+        for j, bank in enumerate(b_banks):
+            nc.scalar.copy(out=b_sb[:, j * N_MM : (j + 1) * N_MM], in_=bank[:])
         old_sb = pool.tile([P, T], F32, name="old_sb", tag="staged")
         nc.sync.dma_start(out=old_sb[:], in_=old)
-        scores(q_raw, "q", a_sb, nc.vector.tensor_copy)
+        a_banks = scores(q_raw, "q", [(nc.vector.tensor_copy, slice(0, 80)), (nc.scalar.copy, slice(80, Q))])
 
         halves = [slice(0, I // 2), slice(I // 2, I)]
         list_halves = [slice(0, I // 32), slice(I // 32, I // 16)]
         b_at1 = pool.tile([P, I], F32, name="b_at1")
         turn = pool.tile([P, I], F32, name="turn")
-        a_at2 = pool.tile([P, I], F32, name="a_at2")
         term = pool.tile([P, I], F32, name="term")
         s = pool.tile([P, I], F32, name="s")
         neg_max = pool.tile([P, 1], F32, name="neg_max")
-        for h, lh in zip(halves, list_halves):
-            nc.scalar.activation(b_at1[:, h], b_sb[:].indirect(list1[:, lh]), ACT.Copy)
+        nc.scalar.activation(b_at1[:, halves[0]], b_sb[:].indirect(list1[:, list_halves[0]]), ACT.Copy)
+        nc.vector.tensor_copy(b_at1[:, halves[1]], b_sb[:].indirect(list1[:, list_halves[1]]))
+        for j, bank in enumerate(a_banks):
+            nc.vector.tensor_copy(out=a_sb[:, j * N_MM : (j + 1) * N_MM], in_=bank[:])
         for h in halves:
             nc.scalar.activation(turn[:, h], b_at1[:, h], ACT.Tanh)
         for h, lh in zip(halves, list_halves):
             nc.scalar.activation(b_at1[:, h], a_sb[:].indirect(list1[:, lh]), ACT.Copy)
         for h, lh in zip(halves, list_halves):
-            nc.vector.tensor_copy(a_at2[:, h], a_sb[:].indirect(list2[:, lh]))
+            nc.vector.tensor_tensor(term[:, h], a_sb[:].indirect(list2[:, lh]), turn[:, h], ALU.mult)
         for h in halves:
-            nc.vector.scalar_tensor_tensor(term[:, h], turn[:, h], lam_sb[:], a_at2[:, h], ALU.mult, ALU.mult)
-        for h in halves:
-            nc.vector.tensor_tensor(s[:, h], term[:, h], b_at1[:, h], ALU.add)
+            nc.vector.scalar_tensor_tensor(s[:, h], term[:, h], lam_sb[:], b_at1[:, h], ALU.mult, ALU.add)
         half_neg_max = pool.tile([P, 2], F32, name="half_neg_max")
         half_sum = pool.tile([P, 2], F32, name="half_sum")
         rescale = pool.tile([P, 2], F32, name="rescale")

from contextlib import ExitStack

import concourse.mybir as mybir

D, T, I, Q = 512, 1024, 512, 128
P = 128
PACK = 4
N_MM = 256
N_OUT = 256

FLOPS = 2 * 2 * D * T * Q

F32 = mybir.dt.float32
BF16 = mybir.dt.bfloat16
I32 = mybir.dt.int32
U32 = mybir.dt.uint32
U16 = mybir.dt.uint16
U8 = mybir.dt.uint8
FP8X4 = mybir.dt.float8_e4m3fn_x4
FP4X4 = mybir.dt.float4_e2m1fn_x4
ACT = mybir.ActivationFunctionType
ALU = mybir.AluOpType


def quantize_query(nc, pool, raw, name, shares):
    grouped = pool.tile([P, Q, PACK], BF16, name=name + "_grouped", align_bytes=64)
    codes = pool.tile([P, Q], U32, name=name + "_codes", align_bytes=64)
    scales = pool.tile([P, Q], U8, name=name + "_scales", align_bytes=64)
    for copy, cols in shares:
        copy(
            out=grouped[:, cols, :].rearrange("p (c i) t -> p c t i", i=4),
            in_=raw[:, :, cols].rearrange("p t (c i) -> p c t i", i=4),
        )
    nc.vector.quantize_mx(
        out=codes[:].bitcast(FP8X4),
        scales=scales[:],
        in_=grouped[:].rearrange("p w t -> p (w t)"),
    )
    return codes, scales


def tile_attend_turnedby_dampened_counts_heads_kernel(
    tc, query, query2, keys_words, keys_scales, lam, damp, old, fade, offs, offs2, out
):
    nc = tc.nc
    with ExitStack() as ctx:
        pool = ctx.enter_context(tc.tile_pool(name="held", bufs=1))
        psum = ctx.enter_context(tc.psum_pool(name="psum", bufs=1))

        list1 = pool.tile([P, I // 16], U16, name="list1")
        list2 = pool.tile([P, I // 16], U16, name="list2")
        q2_raw = pool.tile([P, PACK, Q], F32, name="q2_raw", tag="staged")
        q_raw = pool.tile([P, PACK, Q], F32, name="q_raw")
        words = [pool.tile([P, T], U8, name="words%d" % j, align_bytes=64) for j in range(2)]
        key_scales = pool.tile([P, T], U8, name="key_scales", align_bytes=64)
        lam_sb = pool.tile([P, 1], F32, name="lam_sb")
        damp_sb = pool.tile([P, 1], F32, name="damp_sb")
        fade_sb = pool.tile([P, 1], F32, name="fade_sb")
        placed = pool.tile([P, T], F32, name="placed")

        nc.sync.dma_start(out=q2_raw[:], in_=query2.rearrange("(p t) w -> p t w", t=PACK))
        for quad in range(4):
            nc.scalar.dma_start(
                out=key_scales[32 * quad : 32 * quad + 4, :].bitcast(I32),
                in_=keys_scales[0, 4 * quad : 4 * quad + 4, :].bitcast(I32),
            )
        nc.sync.dma_start(out=words[0][:].bitcast(I32), in_=keys_words[0, :, 0:T].bitcast(I32))
        nc.sync.dma_start(out=q_raw[:], in_=query.rearrange("(p t) w -> p t w", t=PACK))
        nc.sync.dma_start(out=words[1][:].bitcast(I32), in_=keys_words[0, :, T : 2 * T].bitcast(I32))
        nc.sync.dma_start(list1[:], offs)
        nc.sync.dma_start(list2[:], offs2)
        nc.sync.dma_start(out=lam_sb[:], in_=lam)
        nc.sync.dma_start(out=damp_sb[:], in_=damp)
        nc.sync.dma_start(out=fade_sb[:], in_=fade)
        nc.vector.memset(placed[:], 0.0)

        a_sb = pool.tile([P, T], F32, name="a_sb")
        b_sb = pool.tile([P, T], F32, name="b_sb")

        def scores(raw, name, shares):
            codes, scales = quantize_query(nc, pool, raw, name, shares)
            banks = []
            for n0 in range(0, T, N_MM):
                bank = psum.tile([P, N_MM], F32, name="%s_bank%d" % (name, n0 // N_MM))
                nc.tensor.matmul_mx(
                    out=bank[:],
                    lhsT=codes[:].bitcast(FP8X4),
                    lhsT_scale=scales[:],
                    rhs=words[2 * n0 // T][:, 2 * n0 % T : 2 * n0 % T + 2 * N_MM].bitcast(FP4X4),
                    rhs_scale=key_scales[:, n0 : n0 + N_MM],
                    start=True,
                    stop=True,
                )
                banks.append(bank)
            return banks

        b_banks = scores(q2_raw, "q2", [(nc.vector.tensor_copy, slice(0, Q))])
        for j, bank in enumerate(b_banks):
            nc.scalar.copy(out=b_sb[:, j * N_MM : (j + 1) * N_MM], in_=bank[:])
        old_sb = pool.tile([P, T], F32, name="old_sb", tag="staged")
        nc.sync.dma_start(out=old_sb[:], in_=old)
        a_banks = scores(q_raw, "q", [(nc.vector.tensor_copy, slice(0, 80)), (nc.scalar.copy, slice(80, Q))])

        halves = [slice(0, I // 2), slice(I // 2, I)]
        list_halves = [slice(0, I // 32), slice(I // 32, I // 16)]
        b_at1 = pool.tile([P, I], F32, name="b_at1")
        turn = pool.tile([P, I], F32, name="turn")
        term = pool.tile([P, I], F32, name="term")
        s = pool.tile([P, I], F32, name="s")
        neg_max = pool.tile([P, 1], F32, name="neg_max")
        nc.scalar.activation(b_at1[:, halves[0]], b_sb[:].indirect(list1[:, list_halves[0]]), ACT.Copy)
        nc.vector.tensor_copy(b_at1[:, halves[1]], b_sb[:].indirect(list1[:, list_halves[1]]))
        for j, bank in enumerate(a_banks):
            nc.vector.tensor_copy(out=a_sb[:, j * N_MM : (j + 1) * N_MM], in_=bank[:])
        for h in halves:
            nc.scalar.activation(turn[:, h], b_at1[:, h], ACT.Tanh)
        for h, lh in zip(halves, list_halves):
            nc.scalar.activation(b_at1[:, h], a_sb[:].indirect(list1[:, lh]), ACT.Copy)
        for h, lh in zip(halves, list_halves):
            nc.vector.tensor_tensor(term[:, h], a_sb[:].indirect(list2[:, lh]), turn[:, h], ALU.mult)
        for h in halves:
            nc.vector.scalar_tensor_tensor(s[:, h], term[:, h], lam_sb[:], b_at1[:, h], ALU.mult, ALU.add)
        half_neg_max = pool.tile([P, 2], F32, name="half_neg_max")
        half_sum = pool.tile([P, 2], F32, name="half_sum")
        rescale = pool.tile([P, 2], F32, name="rescale")
        rescaled_sum = pool.tile([P, 2], F32, name="rescaled_sum")
        e = pool.tile([P, I], F32, name="e")
        p = pool.tile([P, I], F32, name="p")
        p_sum = pool.tile([P, 1], F32, name="p_sum")
        p_inv = pool.tile([P, 1], F32, name="p_inv")
        gain = pool.tile([P, 1], F32, name="gain")
        for j, h in enumerate(halves):
            nc.vector.tensor_reduce(half_neg_max[:, j : j + 1], s[:, h], mybir.AxisListType.X, ALU.max, negate=True)
        nc.vector.tensor_tensor(neg_max[:], half_neg_max[:, 0:1], half_neg_max[:, 1:2], ALU.min)
        for j, h in enumerate(halves):
            nc.scalar.activation(
                e[:, h], s[:, h], ACT.Exp, bias=half_neg_max[:, j : j + 1], accum_out=half_sum[:, j : j + 1]
            )
        nc.scalar.activation(rescale[:], half_neg_max[:], ACT.Exp, bias=neg_max[:], scale=-1.0)
        nc.vector.scalar_tensor_tensor(
            rescaled_sum[:], half_sum[:], 1.0, rescale[:], ALU.mult, ALU.mult, accum_out=p_sum[:]
        )
        nc.vector.tensor_scalar(p[:, halves[0]], e[:, halves[0]], rescale[:, 0:1], None, ALU.mult)
        nc.vector.reciprocal(p_inv[:], p_sum[:])
        nc.vector.tensor_scalar(p[:, halves[1]], e[:, halves[1]], rescale[:, 1:2], None, ALU.mult)
        nc.vector.tensor_scalar(gain[:], p_inv[:], damp_sb[:], float(I), ALU.mult, ALU.mult)

        part = pool.tile([P, I], F32, name="part")
        part_sum = pool.tile([P, 1], F32, name="part_sum")
        part_inv = pool.tile([P, 1], F32, name="part_inv")
        ws = pool.tile([P, I], F32, name="ws")
        nc.scalar.activation(part[:], p[:], ACT.Ln, bias=1.0, scale=gain[:], accum_out=part_sum[:])
        nc.vector.reciprocal(part_inv[:], part_sum[:])
        nc.vector.tensor_scalar(ws[:], part[:], part_inv[:], float(I), ALU.mult, ALU.mult)
        nc.vector.tensor_copy(placed[:].indirect(list1[:]), ws[:])

        edges = [0, 128, 384, 640, 896, 1024]
        for j in range(len(edges) - 1):
            cols = slice(edges[j], edges[j + 1])
            result = pool.tile([P, edges[j + 1] - edges[j]], F32, name="result%d" % j)
            nc.vector.scalar_tensor_tensor(result[:], old_sb[:, cols], fade_sb[:], placed[:, cols], ALU.mult, ALU.add)
            queue = nc.sync if j % 2 == 0 else nc.scalar
            queue.dma_start(out=out[:, cols], in_=result[:])
